import numpy as np
import ml_dtypes


def mxq(x, axis, fmt="e4m3"):
    dtype, down = {"e4m3": (ml_dtypes.float8_e4m3fn, 7), "e5m2": (ml_dtypes.float8_e5m2, 14)}[fmt]
    v = np.moveaxis(np.asarray(x, np.float32).astype(ml_dtypes.bfloat16).astype(np.float64), axis, -1)
    blocks = v.reshape(v.shape[:-1] + (-1, 32))
    amax = np.abs(blocks).max(-1, keepdims=True)
    byte = np.maximum(np.where(amax > 0, np.frexp(amax)[1] - 1 + 127, 0) - down, 1)
    scale = np.exp2(byte - 127.0)
    codes = (blocks / scale).astype(np.float32).astype(dtype).astype(np.float64)
    return np.moveaxis((codes * scale).reshape(v.shape), -1, axis)


WIDE = False


def mx_kscale(k):
    if not WIDE:
        return np.ones(k)
    levels = np.array([10, -10, 5, -5, 0])
    if k % 512:
        return np.exp2(np.random.permutation(np.resize(levels, k // 32))).repeat(32)
    a = np.empty((k // 512, 16))
    for p in range(k // 512):
        a[p, :8] = np.random.permutation(np.resize(levels, 8))
        for g in range(8):
            far = levels[np.abs(levels - a[p, g]) >= 10]
            a[p, g + 8] = far[np.random.randint(len(far))]
    return np.exp2(a.ravel()).repeat(32)


def f64(x):
    return np.asarray(x).astype(np.float64)


def striped(idx):
    return np.tile(np.asarray(idx).reshape(-1, 16).T, (8, 1)).astype(np.uint16)


def unstriped(offs):
    return offs[:16].T.reshape(-1).astype(np.int64)


E2M1 = np.array([0.0, 0.5, 1.0, 1.5, 2.0, 3.0, 4.0, 6.0, -0.0, -0.5, -1.0, -1.5, -2.0, -3.0, -4.0, -6.0])


def pack_weight(w, fmt):
    k, n = w.shape
    w = f64(np.asarray(w, np.float32).astype(ml_dtypes.bfloat16)).reshape(k // 32, 32, n)
    amax = np.abs(w).max(1)
    if fmt == "e4m3":
        byte = np.frexp(amax)[1] - 1 + 127 - 7
    else:
        mant, ex = np.frexp(amax / 6.0)
        byte = np.where(mant > 0.5, ex, ex - 1) + 127
    byte = np.clip(np.where(amax > 0, byte, 1), 1, 254)
    scaled = (w * np.exp2(127.0 - byte)[:, None, :]).reshape(k, n).astype(np.float32)
    by_word = np.ascontiguousarray(scaled.reshape(k // 512, 128, 4, n).transpose(0, 1, 3, 2))
    if fmt == "e4m3":
        words = by_word.astype(ml_dtypes.float8_e4m3fn).view(np.uint8)
    else:
        c = by_word.astype(ml_dtypes.float4_e2m1fn).view(np.uint8) & 0xF
        words = (c[..., 0::2] | (c[..., 1::2] << 4)).reshape(k // 512, 128, 2 * n)
    return np.ascontiguousarray(words), np.ascontiguousarray(byte.astype(np.uint8).reshape(k // 512, 16, n))


def unpack_weight(words, scales, fmt):
    g, _, n = scales.shape
    words = np.ascontiguousarray(words).reshape(g, 128, n, -1)
    if fmt == "e4m3":
        vals = words.view(ml_dtypes.float8_e4m3fn).astype(np.float64)
    else:
        nib = np.empty((g, 128, n, 4), np.uint8)
        nib[..., 0::2] = words & 0xF
        nib[..., 1::2] = words >> 4
        vals = E2M1[nib]
    vals = vals * np.repeat(np.exp2(scales.astype(np.float64) - 127.0), 8, axis=1)[..., None]
    return vals.transpose(0, 1, 3, 2).reshape(g * 512, n)


def sigmoid(v):
    return 1.0 / (1.0 + np.exp(-v))


D, E, T, I, Q = 512, 512, 2048, 512, 128


def setup_inputs():
    n = np.random.standard_normal
    idx = np.random.permutation(T)[:I]
    fd = mx_kscale(D)
    fe = mx_kscale(E)
    keysp = pack_weight(n((D, T)) / fd[:, None], "e4m3")
    valsp = pack_weight(n((E, T)) / fe[:, None], "e4m3")
    return {
        "query": (n((D, Q)) * 0.8 / np.sqrt(D) * fd[:, None]).astype(np.float32),
        "keys_words": keysp[0],
        "keys_scales": keysp[1],
        "share": (np.random.uniform(0.2, 0.8, (Q, 1))).astype(np.float32),
        "gout": (n((E, Q)) * 1 / np.sqrt(E) * fe[:, None]).astype(np.float32),
        "vals_words": valsp[0],
        "vals_scales": valsp[1],
        "dquery": (n((D, Q)) * 1.0 / np.sqrt(D) * fd[:, None]).astype(np.float32),
        "base": (0.5 * n((Q, T))).astype(np.float32),
        "offs": striped(idx),
    }


def reference(query, keys_words, keys_scales, share, gout, vals_words, vals_scales, dquery, base, offs):
    idx = unstriped(offs)
    keysu = unpack_weight(keys_words, keys_scales, "e4m3")
    valsu = unpack_weight(vals_words, vals_scales, "e4m3")
    queryq = mxq(f64(query), 0, "e4m3")
    keysidxg = keysu[:, idx]
    a = queryq.T @ keysidxg
    dqueryq = mxq(f64(dquery), 0, "e4m3")
    ta = dqueryq.T @ keysidxg
    e0 = np.exp(a)
    s0 = sigmoid(a)
    p = e0 * f64(share) + s0 * (1.0 - f64(share)) * 3.0
    z = np.sum(p, axis=1, keepdims=True)
    goutq = mxq(f64(gout), 0, "e4m3")
    valsidxg = valsu[:, idx]
    c0 = goutq.T @ valsidxg
    dz = np.sum(c0 * p / np.square(z) * (-1.0), axis=1, keepdims=True)
    dp = c0 / z + dz
    ds0 = dp * 3.0 * (1.0 - f64(share))
    de0 = dp * f64(share)
    te0 = ta * e0
    ts0 = ta * s0 * (1.0 - s0)
    tp = te0 * f64(share) + ts0 * (1.0 - f64(share)) * 3.0
    tz = np.sum(tp, axis=1, keepdims=True)
    tdz = np.sum((tp * c0 - tz * z * 2.0 * c0 * p / np.square(z)) / np.square(z) * (-1.0), axis=1, keepdims=True)
    tdp = tz * c0 / np.square(z) * (-1.0) + tdz
    tds0 = tdp * 3.0 * (1.0 - f64(share))
    tde0 = tdp * f64(share)
    tda = (tds0 * s0 + ts0 * ds0) * (1.0 - s0) + ts0 * (-1.0) * ds0 * s0 + tde0 * e0 + te0 * de0
    gs = tda * 512.0
    gf = np.zeros((Q, T))
    gf[:, idx] = gs
    y = f64(base) + gf
    return y

@@ -1,0 +1,153 @@
+from contextlib import ExitStack
+
+import concourse.mybir as mybir
+
+D, E, T, I, Q = 512, 512, 2048, 512, 128
+FLOPS = 3 * 2 * 512 * I * Q
+
+F32 = mybir.dt.float32
+BF16 = mybir.dt.bfloat16
+I32 = mybir.dt.int32
+U32 = mybir.dt.uint32
+U16 = mybir.dt.uint16
+U8 = mybir.dt.uint8
+FP8X4 = mybir.dt.float8_e4m3fn_x4
+ALU = mybir.AluOpType
+ACT = mybir.ActivationFunctionType
+
+P = 128
+PACK = 4
+GAIN = 512.0
+STORE_COLS = 512
+
+
+def tile_attend_hvmixedparts_s_kernel(tc, query, keys_words, keys_scales, share, gout, vals_words, vals_scales, dquery, base, offs, out):
+    nc = tc.nc
+    with ExitStack() as ctx:
+        sb = ctx.enter_context(tc.tile_pool(name="sb", bufs=1))
+        ps = ctx.enter_context(tc.psum_pool(name="ps", bufs=1))
+
+        def slots(name):
+            return sb.tile([P, I], F32, name=name, align_bytes=64)
+
+        def column(name, n=1):
+            return sb.tile([P, n], F32, name=name)
+
+        offsets = sb.tile([P, I // 16], U16, name="offsets")
+        nc.sync.dma_start(offsets[:], offs)
+
+        def load_scales(name, src, clear, queues):
+            plane = sb.tile([P, T], U8, name=name, tag=name, align_bytes=64)
+            clear.memset(plane[:].bitcast(I32), 0)
+            rows = src[0].bitcast(I32)
+            for quad, queue in enumerate(queues):
+                queue.dma_start(plane[32 * quad : 32 * quad + 4, :].bitcast(I32), rows[4 * quad : 4 * quad + 4, :])
+            return plane
+
+        def load_words(name, src, tag):
+            words = sb.tile([P, T], I32, name=name, tag=tag, align_bytes=64)
+            nc.sync.dma_start(words[:], src[0].rearrange("p n t -> p (n t)").bitcast(I32))
+            return words
+
+        def load_rows(name, src, tag):
+            raw = sb.tile([P, PACK, Q], F32, name=name, tag=tag, align_bytes=64)
+            nc.sync.dma_start(raw[:], src.rearrange("(p j) q -> p j q", j=PACK))
+            return raw
+
+        def quantise(name, raw):
+            grouped = sb.tile([P, Q, PACK], BF16, name=name + "_bf16", align_bytes=64)
+            nc.scalar.activation(
+                grouped[:].rearrange("p (c i) t -> p c t i", i=4),
+                raw[:].rearrange("p t (c i) -> p c t i", i=4),
+                ACT.Copy,
+            )
+            codes = sb.tile([P, Q], U32, name=name + "_codes", align_bytes=64)
+            scales = sb.tile([P, Q], U8, name=name + "_scales", align_bytes=64)
+            nc.vector.quantize_mx(out=codes[:].bitcast(FP8X4), scales=scales[:], in_=grouped[:].rearrange("p q t -> p (q t)"))
+            return codes, scales
+
+        def gather(name, window, dtype, tag=None):
+            picked = sb.tile([P, I], dtype, name=name, tag=tag or name, align_bytes=64)
+            nc.vector.tensor_copy(picked[:], window.indirect(offsets[:]))
+            return picked
+
+        def product(name, stationary, words, scales):
+            acc = ps.tile([Q, I], F32, name=name)
+            nc.tensor.matmul_mx(
+                out=acc[:], lhsT=stationary[0][:].bitcast(FP8X4), lhsT_scale=stationary[1][:],
+                rhs=words[:].bitcast(FP8X4), rhs_scale=scales[:], start=True, stop=True,
+            )
+            return acc
+
+        signs = column("signs", 2)
+        nc.gpsimd.memset(signs[:, 0:1], -1.0 / GAIN)
+        nc.gpsimd.memset(signs[:, 1:2], 1.0 / GAIN)
+        half = column("half")
+        nc.gpsimd.memset(half[:], 0.5)
+
+        key_plane = load_scales("key_plane", keys_scales, nc.vector, [nc.scalar] * 4)
+        query_raw = load_rows("query_raw", query, "stage_a")
+        key_pool = load_words("key_pool", keys_words, "stage_b")
+        dquery_raw = load_rows("dquery_raw", dquery, "stage_c")
+        val_plane = load_scales("val_plane", vals_scales, nc.gpsimd, [nc.gpsimd, nc.gpsimd, nc.sync, nc.sync])
+        s = column("s")
+        nc.gpsimd.dma_start(s[:], share)
+
+        placed = sb.tile([P, T], F32, name="placed", align_bytes=64)
+        nc.vector.memset(placed[:], 0.0)
+
+        mix = column("mix", 3)
+        u, u_half, f0_bias = mix[:, 0:1], mix[:, 1:2], mix[:, 2:3]
+        nc.gpsimd.tensor_scalar(u, s[:], -3.0, 3.0, ALU.mult, ALU.add)
+        nc.gpsimd.tensor_scalar(u_half, s[:], -1.5, 1.5, ALU.mult, ALU.add)
+        nc.gpsimd.tensor_scalar(f0_bias, s[:], -0.5, 1.5, ALU.mult, ALU.add)
+
+        key_scales = gather("key_scales", key_plane[:], U8)
+        query_mx = quantise("query", query_raw)
+        val_pool = load_words("val_pool", vals_words, "stage_a")
+        key_words = gather("key_words", key_pool[:].bitcast(U32), U32, "key_plane")
+        a = product("a", query_mx, key_words, key_scales)
+        dquery_mx = quantise("dquery", dquery_raw)
+        gout_raw = load_rows("gout_raw", gout, "stage_c")
+        base_sb = sb.tile([P, T], F32, name="base_sb", tag="stage_b", align_bytes=64)
+        nc.sync.dma_start(base_sb[:], base)
+        ta = product("ta", dquery_mx, key_words, key_scales)
+        val_scales = gather("val_scales", val_plane[:], U8)
+        gout_mx = quantise("gout", gout_raw)
+        val_words = gather("val_words", val_pool[:].bitcast(U32), U32, "val_plane")
+        c = product("c", gout_mx, val_words, val_scales)
+
+        tn, e, rr, f0, f1 = slots("tn"), slots("e"), slots("rr"), slots("f0"), slots("f1")
+        nc.scalar.activation(tn[:], a[:], ACT.Tanh, scale=-0.5)
+        nc.scalar.activation(e[:], a[:], ACT.Exp)
+        nc.scalar.activation(f0[:], tn[:], ACT.Identity, bias=f0_bias, scale=u_half)
+        nc.scalar.activation(rr[:], tn[:], ACT.Square, bias=half[:], scale=0.5)
+        nc.scalar.activation(f1[:], rr[:], ACT.Identity, bias=s[:], scale=u)
+
+        p0, p1, p2, g, tp, w, m = (slots(n) for n in ("p0", "p1", "p2", "g", "tp", "w", "m"))
+        z, k, k2, tau, theta = column("z"), column("k"), column("k2", 2), column("tau"), column("theta", 2)
+        nc.vector.scalar_tensor_tensor(p0[:], f0[:], 1.0 / GAIN, e[:], ALU.mult, ALU.mult, accum_out=z[:])
+        nc.vector.tensor_tensor(p1[:], f1[:], e[:], ALU.mult)
+        nc.vector.reciprocal(k[:], z[:])
+        nc.vector.scalar_tensor_tensor(g[:], f1[:], s[:], tn[:], ALU.subtract, ALU.mult)
+        nc.vector.tensor_scalar(k2[:], signs[:], k[:], None, ALU.mult)
+        nc.vector.scalar_tensor_tensor(tp[:], ta[:], k[:], p1[:], ALU.mult, ALU.mult, accum_out=tau[:])
+        nc.vector.scalar_tensor_tensor(p2[:], g[:], s[:], e[:], ALU.add, ALU.mult)
+
+        mu, b, beta = column("mu"), column("b"), column("beta")
+        cp, ctp, first, second = slots("cp"), slots("ctp"), slots("first"), slots("second")
+        nc.vector.scalar_tensor_tensor(cp[:], c[:], k[:], p0[:], ALU.mult, ALU.mult, accum_out=mu[:])
+        nc.vector.tensor_scalar(theta[:], k2[:], tau[:], None, ALU.mult)
+        nc.vector.scalar_tensor_tensor(ctp[:], c[:], k2[:, 0:1], tp[:], ALU.mult, ALU.mult, accum_out=b[:])
+        nc.vector.scalar_tensor_tensor(w[:], ta[:], k[:], p2[:], ALU.mult, ALU.mult)
+        nc.scalar.activation(beta[:], mu[:], ACT.Identity, bias=b[:], scale=theta[:, 1:2])
+        nc.scalar.activation(second[:], p1[:], ACT.Copy, scale=beta[:])
+        nc.vector.scalar_tensor_tensor(m[:], p1[:], theta[:, 0:1], w[:], ALU.mult, ALU.add)
+        nc.vector.scalar_tensor_tensor(first[:], c[:], mu[:], m[:], ALU.subtract, ALU.mult)
+        nc.vector.tensor_tensor(placed[:].indirect(offsets[:]), first[:], second[:], ALU.add)
+
+        for j in range(T // STORE_COLS):
+            cols = slice(j * STORE_COLS, (j + 1) * STORE_COLS)
+            res = sb.tile([P, STORE_COLS], F32, name=f"res{j}", align_bytes=64)
+            nc.vector.tensor_tensor(res[:], base_sb[:, cols], placed[:, cols], ALU.add)
+            nc.sync.dma_start(out[:, cols], res[:])

@@ -18,7 +18,9 @@ ACT = mybir.ActivationFunctionType
 P = 128
 PACK = 4
 GAIN = 512.0
-STORE_COLS = 512
+HALF = I // 2
+STORE_WIDTHS = (256, 512, 512, 512, 256)
+KEY_ROW, VAL_ROW = 0, 4
 
 
 def tile_attend_hvmixedparts_s_kernel(tc, query, keys_words, keys_scales, share, gout, vals_words, vals_scales, dquery, base, offs, out):
@@ -27,35 +29,33 @@ def tile_attend_hvmixedparts_s_kernel(tc, query, keys_words, keys_scales, share,
         sb = ctx.enter_context(tc.tile_pool(name="sb", bufs=1))
         ps = ctx.enter_context(tc.psum_pool(name="ps", bufs=1))
 
-        def slots(name):
-            return sb.tile([P, I], F32, name=name, align_bytes=64)
+        def slots(name, n=I, tag=None):
+            return sb.tile([P, n], F32, name=name, tag=tag or name, align_bytes=64)
 
         def column(name, n=1):
             return sb.tile([P, n], F32, name=name)
 
-        offsets = sb.tile([P, I // 16], U16, name="offsets")
-        nc.sync.dma_start(offsets[:], offs)
-
-        def load_scales(name, src, clear, queues):
-            plane = sb.tile([P, T], U8, name=name, tag=name, align_bytes=64)
-            clear.memset(plane[:].bitcast(I32), 0)
+        def load_scales(name, src, row, queues):
+            plane = sb.tile([P, T], U8, name=name, align_bytes=64)
+            nc.vector.memset(plane[:].bitcast(I32), 0)
             rows = src[0].bitcast(I32)
             for quad, queue in enumerate(queues):
-                queue.dma_start(plane[32 * quad : 32 * quad + 4, :].bitcast(I32), rows[4 * quad : 4 * quad + 4, :])
+                first = 32 * quad + row
+                queue.dma_start(plane[first : first + 4, :].bitcast(I32), rows[4 * quad : 4 * quad + 4, :])
             return plane
 
-        def load_words(name, src, tag):
-            words = sb.tile([P, T], I32, name=name, tag=tag, align_bytes=64)
+        def load_words(name, src):
+            words = sb.tile([P, T], I32, name=name, tag=name, align_bytes=64)
             nc.sync.dma_start(words[:], src[0].rearrange("p n t -> p (n t)").bitcast(I32))
             return words
 
-        def load_rows(name, src, tag):
-            raw = sb.tile([P, PACK, Q], F32, name=name, tag=tag, align_bytes=64)
+        def load_rows(name, src):
+            raw = sb.tile([P, PACK, Q], F32, name=name, tag=name, align_bytes=64)
             nc.sync.dma_start(raw[:], src.rearrange("(p j) q -> p j q", j=PACK))
             return raw
 
-        def quantise(name, raw):
-            grouped = sb.tile([P, Q, PACK], BF16, name=name + "_bf16", align_bytes=64)
+        def quantise(name, raw, tag):
+            grouped = sb.tile([P, Q, PACK], BF16, name=name + "_bf16", tag=tag, align_bytes=64)
             nc.scalar.activation(
                 grouped[:].rearrange("p (c i) t -> p c t i", i=4),
                 raw[:].rearrange("p t (c i) -> p c t i", i=4),
@@ -64,90 +64,122 @@ def tile_attend_hvmixedparts_s_kernel(tc, query, keys_words, keys_scales, share,
             codes = sb.tile([P, Q], U32, name=name + "_codes", align_bytes=64)
             scales = sb.tile([P, Q], U8, name=name + "_scales", align_bytes=64)
             nc.vector.quantize_mx(out=codes[:].bitcast(FP8X4), scales=scales[:], in_=grouped[:].rearrange("p q t -> p (q t)"))
-            return codes, scales
+            return codes[:], scales[:]
 
-        def gather(name, window, dtype, tag=None):
-            picked = sb.tile([P, I], dtype, name=name, tag=tag or name, align_bytes=64)
+        def gather(name, window, dtype):
+            picked = sb.tile([P, I], dtype, name=name, align_bytes=64)
             nc.vector.tensor_copy(picked[:], window.indirect(offsets[:]))
             return picked
 
         def product(name, stationary, words, scales):
             acc = ps.tile([Q, I], F32, name=name)
             nc.tensor.matmul_mx(
-                out=acc[:], lhsT=stationary[0][:].bitcast(FP8X4), lhsT_scale=stationary[1][:],
-                rhs=words[:].bitcast(FP8X4), rhs_scale=scales[:], start=True, stop=True,
+                out=acc[:], lhsT=stationary[0].bitcast(FP8X4), lhsT_scale=stationary[1],
+                rhs=words[:].bitcast(FP8X4), rhs_scale=scales, start=True, stop=True,
             )
             return acc
 
-        signs = column("signs", 2)
-        nc.gpsimd.memset(signs[:, 0:1], -1.0 / GAIN)
-        nc.gpsimd.memset(signs[:, 1:2], 1.0 / GAIN)
-        half = column("half")
-        nc.gpsimd.memset(half[:], 0.5)
-
-        key_plane = load_scales("key_plane", keys_scales, nc.vector, [nc.scalar] * 4)
-        query_raw = load_rows("query_raw", query, "stage_a")
-        key_pool = load_words("key_pool", keys_words, "stage_b")
-        dquery_raw = load_rows("dquery_raw", dquery, "stage_c")
-        val_plane = load_scales("val_plane", vals_scales, nc.gpsimd, [nc.gpsimd, nc.gpsimd, nc.sync, nc.sync])
+        offsets = sb.tile([P, I // 16], U16, name="offsets")
+        nc.sync.dma_start(offsets[:], offs)
         s = column("s")
-        nc.gpsimd.dma_start(s[:], share)
+        nc.sync.dma_start(s[:], share)
+        query_raw = load_rows("query_raw", query)
+        key_plane = load_scales("key_plane", keys_scales, KEY_ROW, (nc.sync, nc.scalar, nc.sync, nc.scalar))
+        key_pool = load_words("key_pool", keys_words)
+        val_plane = load_scales("val_plane", vals_scales, VAL_ROW, (nc.sync,) * 4)
+        dquery_raw = load_rows("dquery_raw", dquery)
+        val_pool = load_words("val_pool", vals_words)
+        gout_raw = load_rows("gout_raw", gout)
+        base_sb = sb.tile([P, T], F32, name="base_sb", align_bytes=64)
+        nc.sync.dma_start(base_sb[:], base)
 
+        signs = column("signs", 2)
+        nc.vector.memset(signs[:, 0:1], -1.0 / GAIN)
+        nc.vector.memset(signs[:, 1:2], 1.0 / GAIN)
+        half = column("half")
+        nc.vector.memset(half[:], 0.5)
         placed = sb.tile([P, T], F32, name="placed", align_bytes=64)
         nc.vector.memset(placed[:], 0.0)
 
         mix = column("mix", 3)
         u, u_half, f0_bias = mix[:, 0:1], mix[:, 1:2], mix[:, 2:3]
-        nc.gpsimd.tensor_scalar(u, s[:], -3.0, 3.0, ALU.mult, ALU.add)
-        nc.gpsimd.tensor_scalar(u_half, s[:], -1.5, 1.5, ALU.mult, ALU.add)
-        nc.gpsimd.tensor_scalar(f0_bias, s[:], -0.5, 1.5, ALU.mult, ALU.add)
+        nc.vector.tensor_scalar(u, s[:], -3.0, 3.0, ALU.mult, ALU.add)
+        nc.vector.tensor_scalar(u_half, s[:], -1.5, 1.5, ALU.mult, ALU.add)
+        nc.vector.tensor_scalar(f0_bias, s[:], -0.5, 1.5, ALU.mult, ALU.add)
 
         key_scales = gather("key_scales", key_plane[:], U8)
-        query_mx = quantise("query", query_raw)
-        val_pool = load_words("val_pool", vals_words, "stage_a")
-        key_words = gather("key_words", key_pool[:].bitcast(U32), U32, "key_plane")
-        a = product("a", query_mx, key_words, key_scales)
-        dquery_mx = quantise("dquery", dquery_raw)
-        gout_raw = load_rows("gout_raw", gout, "stage_c")
-        base_sb = sb.tile([P, T], F32, name="base_sb", tag="stage_b", align_bytes=64)
-        nc.sync.dma_start(base_sb[:], base)
-        ta = product("ta", dquery_mx, key_words, key_scales)
+        query_mx = quantise("query", query_raw, "query_bf16")
+        key_words = gather("key_words", key_pool[:].bitcast(U32), U32)
+        a = product("a", query_mx, key_words, key_scales[KEY_ROW:, :])
         val_scales = gather("val_scales", val_plane[:], U8)
-        gout_mx = quantise("gout", gout_raw)
-        val_words = gather("val_words", val_pool[:].bitcast(U32), U32, "val_plane")
-        c = product("c", gout_mx, val_words, val_scales)
+        dquery_mx = quantise("dquery", dquery_raw, "dquery_bf16")
+        ta = product("ta", dquery_mx, key_words, key_scales[KEY_ROW:, :])
 
-        tn, e, rr, f0, f1 = slots("tn"), slots("e"), slots("rr"), slots("f0"), slots("f1")
+
+        tn, e, rr, f0, f1 = slots("tn", tag="dquery_raw"), slots("e"), slots("rr"), slots("f0"), slots("f1")
         nc.scalar.activation(tn[:], a[:], ACT.Tanh, scale=-0.5)
         nc.scalar.activation(e[:], a[:], ACT.Exp)
         nc.scalar.activation(f0[:], tn[:], ACT.Identity, bias=f0_bias, scale=u_half)
         nc.scalar.activation(rr[:], tn[:], ACT.Square, bias=half[:], scale=0.5)
         nc.scalar.activation(f1[:], rr[:], ACT.Identity, bias=s[:], scale=u)
 
-        p0, p1, p2, g, tp, w, m = (slots(n) for n in ("p0", "p1", "p2", "g", "tp", "w", "m"))
+        val_words = gather("val_words", val_pool[:].bitcast(U32), U32)
+        gout_mx = quantise("gout", gout_raw, "rr")
+        c = product("c", gout_mx, val_words, val_scales[VAL_ROW:, :])
+
+        p0 = slots("p0", tag="val_pool")
+        tp = slots("tp", tag="rr")
+        p1, cp, ctp = (slots(n) for n in ("p1", "cp", "ctp"))
         z, k, k2, tau, theta = column("z"), column("k"), column("k2", 2), column("tau"), column("theta", 2)
+        mu, b, beta = column("mu"), column("b"), column("beta")
+        halves = (slice(0, HALF), slice(HALF, I))
+        g, p2, w, m, first = ([slots(f"{n}{h}", HALF) for h in range(2)] for n in ("g", "p2_", "w", "m", "first"))
+
+        def make_g(h):
+            nc.vector.scalar_tensor_tensor(g[h][:], f1[:, halves[h]], s[:], tn[:, halves[h]], ALU.subtract, ALU.mult)
+
+        def make_p2(h):
+            nc.vector.scalar_tensor_tensor(p2[h][:], g[h][:], s[:], e[:, halves[h]], ALU.add, ALU.mult)
+
+        def make_w(h):
+            nc.vector.scalar_tensor_tensor(w[h][:], ta[:, halves[h]], k[:], p2[h][:], ALU.mult, ALU.mult)
+
+        def make_m(h):
+            nc.vector.scalar_tensor_tensor(m[h][:], p1[:, halves[h]], theta[:, 0:1], w[h][:], ALU.mult, ALU.add)
+
+        def make_first(h):
+            nc.vector.scalar_tensor_tensor(first[h][:], c[:, halves[h]], mu[:], m[h][:], ALU.subtract, ALU.mult)
+
         nc.vector.scalar_tensor_tensor(p0[:], f0[:], 1.0 / GAIN, e[:], ALU.mult, ALU.mult, accum_out=z[:])
         nc.vector.tensor_tensor(p1[:], f1[:], e[:], ALU.mult)
         nc.vector.reciprocal(k[:], z[:])
-        nc.vector.scalar_tensor_tensor(g[:], f1[:], s[:], tn[:], ALU.subtract, ALU.mult)
-        nc.vector.tensor_scalar(k2[:], signs[:], k[:], None, ALU.mult)
+        nc.scalar.activation(k2[:], signs[:], ACT.Copy, scale=k[:])
+        make_g(0)
         nc.vector.scalar_tensor_tensor(tp[:], ta[:], k[:], p1[:], ALU.mult, ALU.mult, accum_out=tau[:])
-        nc.vector.scalar_tensor_tensor(p2[:], g[:], s[:], e[:], ALU.add, ALU.mult)
-
-        mu, b, beta = column("mu"), column("b"), column("beta")
-        cp, ctp, first, second = slots("cp"), slots("ctp"), slots("first"), slots("second")
+        nc.scalar.activation(theta[:], k2[:], ACT.Copy, scale=tau[:])
+        make_p2(0)
         nc.vector.scalar_tensor_tensor(cp[:], c[:], k[:], p0[:], ALU.mult, ALU.mult, accum_out=mu[:])
-        nc.vector.tensor_scalar(theta[:], k2[:], tau[:], None, ALU.mult)
+        make_w(0)
         nc.vector.scalar_tensor_tensor(ctp[:], c[:], k2[:, 0:1], tp[:], ALU.mult, ALU.mult, accum_out=b[:])
-        nc.vector.scalar_tensor_tensor(w[:], ta[:], k[:], p2[:], ALU.mult, ALU.mult)
+        make_m(0)
         nc.scalar.activation(beta[:], mu[:], ACT.Identity, bias=b[:], scale=theta[:, 1:2])
-        nc.scalar.activation(second[:], p1[:], ACT.Copy, scale=beta[:])
-        nc.vector.scalar_tensor_tensor(m[:], p1[:], theta[:, 0:1], w[:], ALU.mult, ALU.add)
-        nc.vector.scalar_tensor_tensor(first[:], c[:], mu[:], m[:], ALU.subtract, ALU.mult)
-        nc.vector.tensor_tensor(placed[:].indirect(offsets[:]), first[:], second[:], ALU.add)
+        second = slots("second", HALF)
+        nc.scalar.activation(second[:], p1[:, halves[1]], ACT.Copy, scale=beta[:])
+        make_g(1)
+        make_first(0)
+        make_p2(1)
+        gs = slots("gs", HALF)
+        nc.vector.scalar_tensor_tensor(gs[:], p1[:, halves[0]], beta[:], first[0][:], ALU.mult, ALU.add)
+        nc.scalar.activation(placed[:].indirect(offsets[:, : HALF // 16]), gs[:], ACT.Copy)
+        make_w(1)
+        make_m(1)
+        make_first(1)
+        nc.vector.tensor_tensor(placed[:].indirect(offsets[:, HALF // 16 :]), first[1][:], second[:], ALU.add)
 
-        for j in range(T // STORE_COLS):
-            cols = slice(j * STORE_COLS, (j + 1) * STORE_COLS)
-            res = sb.tile([P, STORE_COLS], F32, name=f"res{j}", align_bytes=64)
+        start = 0
+        for j, width in enumerate(STORE_WIDTHS):
+            cols = slice(start, start + width)
+            start += width
+            res = slots(f"res{j}", width)
             nc.vector.tensor_tensor(res[:], base_sb[:, cols], placed[:, cols], ALU.add)
             nc.sync.dma_start(out[:, cols], res[:])

from contextlib import ExitStack

import concourse.mybir as mybir

D, E, T, I, Q = 512, 512, 2048, 512, 128
FLOPS = 3 * 2 * 512 * I * Q

F32 = mybir.dt.float32
BF16 = mybir.dt.bfloat16
I32 = mybir.dt.int32
U32 = mybir.dt.uint32
U16 = mybir.dt.uint16
U8 = mybir.dt.uint8
FP8X4 = mybir.dt.float8_e4m3fn_x4
ALU = mybir.AluOpType
ACT = mybir.ActivationFunctionType

P = 128
PACK = 4
GAIN = 512.0
HALF = I // 2
STORE_WIDTHS = (256, 512, 512, 512, 256)
KEY_ROW, VAL_ROW = 0, 4


def tile_attend_hvmixedparts_s_kernel(tc, query, keys_words, keys_scales, share, gout, vals_words, vals_scales, dquery, base, offs, out):
    nc = tc.nc
    with ExitStack() as ctx:
        sb = ctx.enter_context(tc.tile_pool(name="sb", bufs=1))
        ps = ctx.enter_context(tc.psum_pool(name="ps", bufs=1))

        def slots(name, n=I, tag=None):
            return sb.tile([P, n], F32, name=name, tag=tag or name, align_bytes=64)

        def column(name, n=1):
            return sb.tile([P, n], F32, name=name)

        def load_scales(name, src, row, queues):
            plane = sb.tile([P, T], U8, name=name, align_bytes=64)
            nc.vector.memset(plane[:].bitcast(I32), 0)
            rows = src[0].bitcast(I32)
            for quad, queue in enumerate(queues):
                first = 32 * quad + row
                queue.dma_start(plane[first : first + 4, :].bitcast(I32), rows[4 * quad : 4 * quad + 4, :])
            return plane

        def load_words(name, src):
            words = sb.tile([P, T], I32, name=name, tag=name, align_bytes=64)
            nc.sync.dma_start(words[:], src[0].rearrange("p n t -> p (n t)").bitcast(I32))
            return words

        def load_rows(name, src):
            raw = sb.tile([P, PACK, Q], F32, name=name, tag=name, align_bytes=64)
            nc.sync.dma_start(raw[:], src.rearrange("(p j) q -> p j q", j=PACK))
            return raw

        def quantise(name, raw, tag):
            grouped = sb.tile([P, Q, PACK], BF16, name=name + "_bf16", tag=tag, align_bytes=64)
            nc.scalar.activation(
                grouped[:].rearrange("p (c i) t -> p c t i", i=4),
                raw[:].rearrange("p t (c i) -> p c t i", i=4),
                ACT.Copy,
            )
            codes = sb.tile([P, Q], U32, name=name + "_codes", align_bytes=64)
            scales = sb.tile([P, Q], U8, name=name + "_scales", align_bytes=64)
            nc.vector.quantize_mx(out=codes[:].bitcast(FP8X4), scales=scales[:], in_=grouped[:].rearrange("p q t -> p (q t)"))
            return codes[:], scales[:]

        def gather(name, window, dtype):
            picked = sb.tile([P, I], dtype, name=name, align_bytes=64)
            nc.vector.tensor_copy(picked[:], window.indirect(offsets[:]))
            return picked

        def product(name, stationary, words, scales):
            acc = ps.tile([Q, I], F32, name=name)
            nc.tensor.matmul_mx(
                out=acc[:], lhsT=stationary[0].bitcast(FP8X4), lhsT_scale=stationary[1],
                rhs=words[:].bitcast(FP8X4), rhs_scale=scales, start=True, stop=True,
            )
            return acc

        offsets = sb.tile([P, I // 16], U16, name="offsets")
        nc.sync.dma_start(offsets[:], offs)
        s = column("s")
        nc.sync.dma_start(s[:], share)
        query_raw = load_rows("query_raw", query)
        key_plane = load_scales("key_plane", keys_scales, KEY_ROW, (nc.sync, nc.scalar, nc.sync, nc.scalar))
        key_pool = load_words("key_pool", keys_words)
        val_plane = load_scales("val_plane", vals_scales, VAL_ROW, (nc.sync,) * 4)
        dquery_raw = load_rows("dquery_raw", dquery)
        val_pool = load_words("val_pool", vals_words)
        gout_raw = load_rows("gout_raw", gout)
        base_sb = sb.tile([P, T], F32, name="base_sb", align_bytes=64)
        nc.sync.dma_start(base_sb[:], base)

        signs = column("signs", 2)
        nc.vector.memset(signs[:, 0:1], -1.0 / GAIN)
        nc.vector.memset(signs[:, 1:2], 1.0 / GAIN)
        half = column("half")
        nc.vector.memset(half[:], 0.5)
        placed = sb.tile([P, T], F32, name="placed", align_bytes=64)
        nc.vector.memset(placed[:], 0.0)

        mix = column("mix", 3)
        u, u_half, f0_bias = mix[:, 0:1], mix[:, 1:2], mix[:, 2:3]
        nc.vector.tensor_scalar(u, s[:], -3.0, 3.0, ALU.mult, ALU.add)
        nc.vector.tensor_scalar(u_half, s[:], -1.5, 1.5, ALU.mult, ALU.add)
        nc.vector.tensor_scalar(f0_bias, s[:], -0.5, 1.5, ALU.mult, ALU.add)

        key_scales = gather("key_scales", key_plane[:], U8)
        query_mx = quantise("query", query_raw, "query_bf16")
        key_words = gather("key_words", key_pool[:].bitcast(U32), U32)
        a = product("a", query_mx, key_words, key_scales[KEY_ROW:, :])
        val_scales = gather("val_scales", val_plane[:], U8)
        dquery_mx = quantise("dquery", dquery_raw, "dquery_bf16")
        ta = product("ta", dquery_mx, key_words, key_scales[KEY_ROW:, :])


        tn, e, rr, f0, f1 = slots("tn", tag="dquery_raw"), slots("e"), slots("rr"), slots("f0"), slots("f1")
        nc.scalar.activation(tn[:], a[:], ACT.Tanh, scale=-0.5)
        nc.scalar.activation(e[:], a[:], ACT.Exp)
        nc.scalar.activation(f0[:], tn[:], ACT.Identity, bias=f0_bias, scale=u_half)
        nc.scalar.activation(rr[:], tn[:], ACT.Square, bias=half[:], scale=0.5)
        nc.scalar.activation(f1[:], rr[:], ACT.Identity, bias=s[:], scale=u)

        val_words = gather("val_words", val_pool[:].bitcast(U32), U32)
        gout_mx = quantise("gout", gout_raw, "rr")
        c = product("c", gout_mx, val_words, val_scales[VAL_ROW:, :])

        p0 = slots("p0", tag="val_pool")
        tp = slots("tp", tag="rr")
        p1, cp, ctp = (slots(n) for n in ("p1", "cp", "ctp"))
        z, k, k2, tau, theta = column("z"), column("k"), column("k2", 2), column("tau"), column("theta", 2)
        mu, b, beta = column("mu"), column("b"), column("beta")
        halves = (slice(0, HALF), slice(HALF, I))
        g, p2, w, m, first = ([slots(f"{n}{h}", HALF) for h in range(2)] for n in ("g", "p2_", "w", "m", "first"))

        def make_g(h):
            nc.vector.scalar_tensor_tensor(g[h][:], f1[:, halves[h]], s[:], tn[:, halves[h]], ALU.subtract, ALU.mult)

        def make_p2(h):
            nc.vector.scalar_tensor_tensor(p2[h][:], g[h][:], s[:], e[:, halves[h]], ALU.add, ALU.mult)

        def make_w(h):
            nc.vector.scalar_tensor_tensor(w[h][:], ta[:, halves[h]], k[:], p2[h][:], ALU.mult, ALU.mult)

        def make_m(h):
            nc.vector.scalar_tensor_tensor(m[h][:], p1[:, halves[h]], theta[:, 0:1], w[h][:], ALU.mult, ALU.add)

        def make_first(h):
            nc.vector.scalar_tensor_tensor(first[h][:], c[:, halves[h]], mu[:], m[h][:], ALU.subtract, ALU.mult)

        nc.vector.scalar_tensor_tensor(p0[:], f0[:], 1.0 / GAIN, e[:], ALU.mult, ALU.mult, accum_out=z[:])
        nc.vector.tensor_tensor(p1[:], f1[:], e[:], ALU.mult)
        nc.vector.reciprocal(k[:], z[:])
        nc.scalar.activation(k2[:], signs[:], ACT.Copy, scale=k[:])
        make_g(0)
        nc.vector.scalar_tensor_tensor(tp[:], ta[:], k[:], p1[:], ALU.mult, ALU.mult, accum_out=tau[:])
        nc.scalar.activation(theta[:], k2[:], ACT.Copy, scale=tau[:])
        make_p2(0)
        nc.vector.scalar_tensor_tensor(cp[:], c[:], k[:], p0[:], ALU.mult, ALU.mult, accum_out=mu[:])
        make_w(0)
        nc.vector.scalar_tensor_tensor(ctp[:], c[:], k2[:, 0:1], tp[:], ALU.mult, ALU.mult, accum_out=b[:])
        make_m(0)
        nc.scalar.activation(beta[:], mu[:], ACT.Identity, bias=b[:], scale=theta[:, 1:2])
        second = slots("second", HALF)
        nc.scalar.activation(second[:], p1[:, halves[1]], ACT.Copy, scale=beta[:])
        make_g(1)
        make_first(0)
        make_p2(1)
        gs = slots("gs", HALF)
        nc.vector.scalar_tensor_tensor(gs[:], p1[:, halves[0]], beta[:], first[0][:], ALU.mult, ALU.add)
        nc.scalar.activation(placed[:].indirect(offsets[:, : HALF // 16]), gs[:], ACT.Copy)
        make_w(1)
        make_m(1)
        make_first(1)
        nc.vector.tensor_tensor(placed[:].indirect(offsets[:, HALF // 16 :]), first[1][:], second[:], ALU.add)

        start = 0
        for j, width in enumerate(STORE_WIDTHS):
            cols = slice(start, start + width)
            start += width
            res = slots(f"res{j}", width)
            nc.vector.tensor_tensor(res[:], base_sb[:, cols], placed[:, cols], ALU.add)
            nc.sync.dma_start(out[:, cols], res[:])
